import numpy as np
import ml_dtypes


def mxq(x, axis, fmt="e4m3"):
    dtype, down = {"e4m3": (ml_dtypes.float8_e4m3fn, 7), "e5m2": (ml_dtypes.float8_e5m2, 14)}[fmt]
    v = np.moveaxis(np.asarray(x, np.float32).astype(ml_dtypes.bfloat16).astype(np.float64), axis, -1)
    blocks = v.reshape(v.shape[:-1] + (-1, 32))
    amax = np.abs(blocks).max(-1, keepdims=True)
    byte = np.maximum(np.where(amax > 0, np.frexp(amax)[1] - 1 + 127, 0) - down, 1)
    scale = np.exp2(byte - 127.0)
    codes = (blocks / scale).astype(np.float32).astype(dtype).astype(np.float64)
    return np.moveaxis((codes * scale).reshape(v.shape), -1, axis)


WIDE = False


def mx_kscale(k):
    if not WIDE:
        return np.ones(k)
    levels = np.array([10, -10, 5, -5, 0])
    if k % 512:
        return np.exp2(np.random.permutation(np.resize(levels, k // 32))).repeat(32)
    a = np.empty((k // 512, 16))
    for p in range(k // 512):
        a[p, :8] = np.random.permutation(np.resize(levels, 8))
        for g in range(8):
            far = levels[np.abs(levels - a[p, g]) >= 10]
            a[p, g + 8] = far[np.random.randint(len(far))]
    return np.exp2(a.ravel()).repeat(32)


def f64(x):
    return np.asarray(x).astype(np.float64)


def striped(idx):
    return np.tile(np.asarray(idx).reshape(-1, 16).T, (8, 1)).astype(np.uint16)


def unstriped(offs):
    return offs[:16].T.reshape(-1).astype(np.int64)


E2M1 = np.array([0.0, 0.5, 1.0, 1.5, 2.0, 3.0, 4.0, 6.0, -0.0, -0.5, -1.0, -1.5, -2.0, -3.0, -4.0, -6.0])


def pack_weight(w, fmt):
    k, n = w.shape
    w = f64(np.asarray(w, np.float32).astype(ml_dtypes.bfloat16)).reshape(k // 32, 32, n)
    amax = np.abs(w).max(1)
    if fmt == "e4m3":
        byte = np.frexp(amax)[1] - 1 + 127 - 7
    else:
        mant, ex = np.frexp(amax / 6.0)
        byte = np.where(mant > 0.5, ex, ex - 1) + 127
    byte = np.clip(np.where(amax > 0, byte, 1), 1, 254)
    scaled = (w * np.exp2(127.0 - byte)[:, None, :]).reshape(k, n).astype(np.float32)
    by_word = np.ascontiguousarray(scaled.reshape(k // 512, 128, 4, n).transpose(0, 1, 3, 2))
    if fmt == "e4m3":
        words = by_word.astype(ml_dtypes.float8_e4m3fn).view(np.uint8)
    else:
        c = by_word.astype(ml_dtypes.float4_e2m1fn).view(np.uint8) & 0xF
        words = (c[..., 0::2] | (c[..., 1::2] << 4)).reshape(k // 512, 128, 2 * n)
    return np.ascontiguousarray(words), np.ascontiguousarray(byte.astype(np.uint8).reshape(k // 512, 16, n))


def unpack_weight(words, scales, fmt):
    g, _, n = scales.shape
    words = np.ascontiguousarray(words).reshape(g, 128, n, -1)
    if fmt == "e4m3":
        vals = words.view(ml_dtypes.float8_e4m3fn).astype(np.float64)
    else:
        nib = np.empty((g, 128, n, 4), np.uint8)
        nib[..., 0::2] = words & 0xF
        nib[..., 1::2] = words >> 4
        vals = E2M1[nib]
    vals = vals * np.repeat(np.exp2(scales.astype(np.float64) - 127.0), 8, axis=1)[..., None]
    return vals.transpose(0, 1, 3, 2).reshape(g * 512, n)


def bf(x):
    return np.asarray(x, np.float32).astype(ml_dtypes.bfloat16)


def planes(Y):
    r, m = Y.shape
    b = f64(bf(Y)).reshape(r // 32, 32, m)
    amax = np.abs(b).max(1)
    byte = np.clip(np.where(amax > 0, np.frexp(amax)[1] - 1 + 127 - 7, 1), 1, 254)
    codes = (b * np.exp2(127.0 - byte)[:, None, :]).reshape(r, m).astype(np.float32).astype(ml_dtypes.float8_e4m3fn).view(np.uint8)
    words = codes.reshape(r // 512, 128, 4, m).transpose(0, 1, 3, 2)
    return np.ascontiguousarray(words), np.ascontiguousarray(byte.astype(np.uint8).reshape(r // 512, 16, m))


D, T, I, Q, G, E = 512, 2048, 512, 256, 32, 512


def setup_inputs():
    n = np.random.standard_normal
    idx = np.random.permutation(T)[:I]
    fd = mx_kscale(D)
    fi = mx_kscale(I)
    ti = np.ones(T)
    ti[idx] = fi
    keysp = pack_weight(n((D, T)) / fd[:, None], "e2m1")
    return {
        "query": (n((D, Q)) * 0.7 / np.sqrt(D) * fd[:, None]).astype(np.float32),
        "keys_words": keysp[0],
        "keys_scales": keysp[1],
        "reserve": (np.random.uniform(1.0, 8.0, (I, 1))).astype(np.float32),
        "us": (np.random.uniform(0.1, 0.4, (I, 1)) * fi[:, None]).astype(np.float32),
        "vals": (n((E, T)) / ti).astype(np.float32),
        "offs": striped(idx),
    }


def reference(query, keys_words, keys_scales, reserve, us, vals, offs):
    idx = unstriped(offs)
    keysu = unpack_weight(keys_words, keys_scales, "e2m1")
    keysidxg = keysu[:, idx]
    queryq = mxq(f64(query), 0, "e4m3")
    a = keysidxg.T @ queryq
    p = np.exp(a)
    b = f64(us) / (p.reshape(I, G, Q // G).sum(axis=2) + f64(reserve))
    br = np.repeat(b, Q // G, axis=1)
    w = p * br
    vt = f64(vals)[:, idx].T
    vtq = mxq(vt, 0, "e4m3")
    wq = mxq(w, 0, "e4m3")
    o = vtq.T @ wq
    words, scales = planes(o)
    return o, words, scales

@@ -1,0 +1,222 @@
+from contextlib import ExitStack
+
+import concourse.mybir as mybir
+from concourse.masks import make_identity
+
+D, T, I, Q, G, E = 512, 2048, 512, 256, 32, 512
+FLOPS = 2 * D * I * Q + 2 * I * E * Q
+
+F32 = mybir.dt.float32
+BF16 = mybir.dt.bfloat16
+I32 = mybir.dt.int32
+U32 = mybir.dt.uint32
+U16 = mybir.dt.uint16
+U8 = mybir.dt.uint8
+FP8X4 = mybir.dt.float8_e4m3fn_x4
+FP4X4 = mybir.dt.float4_e2m1fn_x4
+EXP = mybir.ActivationFunctionType.Exp
+MULT = mybir.AluOpType.mult
+
+P = 128
+PACK = 4
+TEAM = Q // G
+HALVES = 2
+QH = Q // HALVES
+GH = G // HALVES
+
+
+def tile_attend_teamshares_pl_kernel(tc, query, keys_words, keys_scales, reserve, us, vals, offs, out_0, out_1, out_2):
+    nc = tc.nc
+    with ExitStack() as ctx:
+        sb = ctx.enter_context(tc.tile_pool(name="sb", bufs=1))
+        ps = ctx.enter_context(tc.psum_pool(name="ps", bufs=1))
+        turn = ctx.enter_context(tc.psum_pool(name="turn", bufs=2))
+
+        offsets = sb.tile([P, I // 16], U16, name="offsets")
+        nc.sync.dma_start(offsets[:], offs)
+
+        pool_words = sb.tile([P, T], U16, name="pool_words", align_bytes=64)
+        nc.sync.dma_start(pool_words[:].bitcast(I32), keys_words[0].bitcast(I32))
+
+        pool_scales = sb.tile([P, T], U8, name="pool_scales", align_bytes=64)
+        nc.gpsimd.memset(pool_scales[:].bitcast(I32), 0)
+        identity = sb.tile([P, P], F32, name="identity")
+        make_identity(nc, identity[:])
+        warm_in = sb.tile([P, 8], F32, name="warm_in")
+        nc.vector.memset(warm_in[:], 0.0)
+
+        for quad in range(4):
+            nc.sync.dma_start(
+                pool_scales[32 * quad : 32 * quad + 4, :].bitcast(I32),
+                keys_scales[0, 4 * quad : 4 * quad + 4, :].bitcast(I32),
+            )
+        q_raw = sb.tile([P, PACK, Q], F32, name="q_raw")
+        nc.sync.dma_start(q_raw[:], query.rearrange("(p j) q -> p j q", j=PACK))
+        vals_rows = vals.rearrange("(p j) t -> j p t", j=PACK)
+        pool_vals = [sb.tile([P, T], F32, name="pool_vals%d" % j, align_bytes=64) for j in range(PACK)]
+        reserve_sb = sb.tile([P, PACK], F32, name="reserve_sb")
+        us_sb = sb.tile([P, PACK], F32, name="us_sb")
+        nc.sync.dma_start(pool_vals[0][:], vals_rows[0])
+        nc.sync.dma_start(reserve_sb[:], reserve.rearrange("(p r) o -> p (r o)", r=PACK))
+        nc.sync.dma_start(us_sb[:], us.rearrange("(p r) o -> p (r o)", r=PACK))
+        for j in range(1, PACK):
+            nc.sync.dma_start(pool_vals[j][:], vals_rows[j])
+
+        warm_out = sb.tile([P, 8], F32, name="warm_out")
+        nc.scalar.activation(warm_out[:], warm_in[:], EXP)
+
+        got_scales = sb.tile([P, I], U8, name="got_scales", align_bytes=64)
+        nc.vector.tensor_copy(got_scales[:], pool_scales[:].indirect(offsets[:]))
+        got_words = sb.tile([P, I], U16, name="got_words", align_bytes=64)
+        nc.vector.tensor_copy(got_words[:], pool_words[:].indirect(offsets[:]))
+        k_scales = sb.tile([P, I], U8, name="k_scales", align_bytes=64)
+        nc.vector.tensor_copy(
+            k_scales[:].rearrange("p (r s) -> p s r", r=PACK), got_scales[:].rearrange("p (s r) -> p s r", r=PACK)
+        )
+        k_words = sb.tile([P, I], U16, name="k_words", align_bytes=64)
+        nc.vector.tensor_copy(
+            k_words[:].rearrange("p (r s) -> p s r", r=PACK), got_words[:].rearrange("p (s r) -> p s r", r=PACK)
+        )
+
+        q_bf = sb.tile([P, Q, PACK], BF16, name="q_bf", align_bytes=64)
+        nc.scalar.copy(q_bf[:], q_raw[:].rearrange("p j q -> p q j"))
+        q_codes = sb.tile([P, Q], U32, name="q_codes", align_bytes=64)
+        q_scales = sb.tile([P, Q], U8, name="q_scales", align_bytes=64)
+        nc.vector.quantize_mx(q_codes[:].bitcast(FP8X4), q_scales[:], q_bf[:].rearrange("p q j -> p (q j)"))
+
+        reserve_wide = sb.tile([P, G, PACK], F32, name="reserve_wide")
+        nc.scalar.copy(reserve_wide[:], reserve_sb[:].unsqueeze(1).to_broadcast([P, G, PACK]))
+
+        p_sb = sb.tile([P, TEAM, G * PACK], F32, name="p_sb", align_bytes=64)
+        for h in range(HALVES):
+            scores = ps.tile([P, PACK, QH], F32, name="scores%d" % h)
+            cols = slice(h * QH, (h + 1) * QH)
+            for r in range(PACK):
+                slots = slice(r * P, (r + 1) * P)
+                nc.tensor.matmul_mx(
+                    scores[:, r, :],
+                    lhsT=k_words[:, slots].bitcast(FP4X4),
+                    lhsT_scale=k_scales[:, slots],
+                    rhs=q_codes[:, cols].bitcast(FP8X4),
+                    rhs_scale=q_scales[:, cols],
+                    start=True,
+                    stop=True,
+                )
+            nc.scalar.activation(
+                p_sb[:, :, h * GH * PACK : (h + 1) * GH * PACK].rearrange("p u (g r) -> p u g r", r=PACK),
+                scores[:].rearrange("p r (g u) -> p u g r", u=TEAM),
+                EXP,
+            )
+
+        def gather_and_turn(j):
+            got = sb.tile([P, I], BF16, name="got_vals%d" % j, align_bytes=64)
+            nc.vector.tensor_copy(got[:], pool_vals[j][:].indirect(offsets[:]))
+            pairs = got[:].bitcast(F32)
+            turned = turn.tile([P, 2, P], F32, name="turned")
+            for u in range(2):
+                nc.tensor.transpose(turned[:, u, :], pairs[:, u : I // 2 : 2], identity[:])
+            v_bf = sb.tile([P, P, PACK], BF16, name="v_bf%d" % j, align_bytes=64)
+            nc.scalar.copy(
+                v_bf[:].rearrange("p m t -> p (m t)").bitcast(F32).rearrange("p (m u) -> p m u", u=2),
+                turned[:].rearrange("p u m -> p m u"),
+            )
+            return v_bf
+
+        def quantize_vals(j, v_bf):
+            codes = sb.tile([P, P], U32, name="v_codes%d" % j, align_bytes=64)
+            scales = sb.tile([P, P], U8, name="v_scales%d" % j, align_bytes=64)
+            nc.vector.quantize_mx(codes[:].bitcast(FP8X4), scales[:], v_bf[:].rearrange("p m t -> p (m t)"))
+            return codes, scales
+
+        v_ops = []
+        v_bf0 = gather_and_turn(0)
+
+        den_t = ps.tile([P, P], F32, name="den_t")
+        nc.tensor.matmul(
+            den_t[:], reserve_wide[:].rearrange("p g r -> p (g r)"), identity[:], start=True, stop=False, is_transpose=True
+        )
+        for u in range(TEAM):
+            nc.tensor.matmul(den_t[:], p_sb[:, u, :], identity[:], start=False, stop=(u == TEAM - 1), is_transpose=True)
+        v_ops.append(quantize_vals(0, v_bf0))
+        rec_t = sb.tile([P, P], F32, name="rec_t")
+        nc.vector.reciprocal(rec_t[:], den_t[:])
+        rec = ps.tile([P, P], F32, name="rec")
+        nc.tensor.transpose(rec[:], rec_t[:], identity[:])
+        v_bf1 = gather_and_turn(1)
+        b_sb = sb.tile([P, G, PACK], F32, name="b_sb")
+        nc.vector.tensor_tensor(
+            b_sb[:],
+            rec[:].rearrange("p (g r) -> p g r", r=PACK),
+            us_sb[:].unsqueeze(1).to_broadcast([P, G, PACK]),
+            MULT,
+        )
+        v_ops.append(quantize_vals(1, v_bf1))
+
+        w_bf, w_codes, w_scales = [], [], []
+        for h in range(HALVES):
+            part = slice(h * GH * PACK, (h + 1) * GH * PACK)
+            w_h = sb.tile([P, TEAM, GH * PACK], BF16, name="w_bf%d" % h, align_bytes=64)
+            nc.vector.tensor_tensor(
+                w_h[:],
+                p_sb[:, :, part],
+                b_sb[:].rearrange("p g r -> p (g r)")[:, part].unsqueeze(1).to_broadcast([P, TEAM, GH * PACK]),
+                MULT,
+            )
+            w_bf.append(w_h)
+        for h in range(HALVES):
+            codes = sb.tile([P, QH], U32, name="w_codes%d" % h, align_bytes=64)
+            scales = sb.tile([P, QH], U8, name="w_scales%d" % h, align_bytes=64)
+            nc.vector.quantize_mx(codes[:].bitcast(FP8X4), scales[:], w_bf[h][:].rearrange("p u x -> p (u x)"))
+            w_codes.append(codes)
+            w_scales.append(scales)
+
+        v_ops.append(quantize_vals(2, gather_and_turn(2)))
+
+        sums = [ps.tile([P, PACK, QH], F32, name="sums%d" % h) for h in range(HALVES)]
+        out_rows = out_0.rearrange("(p j) q -> p j q", j=PACK)
+
+        def product(j):
+            for h in range(HALVES):
+                nc.tensor.matmul_mx(
+                    sums[h][:, j, :],
+                    lhsT=v_ops[j][0][:].bitcast(FP8X4),
+                    lhsT_scale=v_ops[j][1][:],
+                    rhs=w_codes[h][:].bitcast(FP8X4),
+                    rhs_scale=w_scales[h][:],
+                    start=True,
+                    stop=True,
+                )
+
+        def store_rows(first, count):
+            o_sb = sb.tile([P, count, Q], F32, name="o_sb%d" % first)
+            for h in range(HALVES):
+                nc.scalar.copy(
+                    o_sb[:, :, h * QH : (h + 1) * QH].rearrange("p j (g u) -> p j g u", u=TEAM),
+                    sums[h][:, first : first + count, :].rearrange("p j (u g) -> p j g u", u=TEAM),
+                )
+            nc.sync.dma_start(out_rows[:, first : first + count, :], o_sb[:])
+
+        for j in range(PACK - 1):
+            product(j)
+        store_rows(0, PACK - 1)
+
+        v_ops.append(quantize_vals(3, gather_and_turn(3)))
+        product(PACK - 1)
+
+        y_bf = sb.tile([P, Q, PACK], BF16, name="y_bf", align_bytes=64)
+        for h, copy in enumerate((nc.vector.tensor_copy, nc.scalar.copy)):
+            copy(
+                y_bf[:, h * QH : (h + 1) * QH, :].rearrange("p (g u) j -> p g u j", u=TEAM),
+                sums[h][:].rearrange("p j (u g) -> p g u j", u=TEAM),
+            )
+        store_rows(PACK - 1, 1)
+        y_codes = sb.tile([P, Q], U32, name="y_codes", align_bytes=64)
+        y_scales = sb.tile([P, Q], U8, name="y_scales", align_bytes=64)
+        nc.vector.quantize_mx(y_codes[:].bitcast(FP8X4), y_scales[:], y_bf[:].rearrange("p q j -> p (q j)"))
+        nc.sync.dma_start(out_1[0].rearrange("p q j -> p (q j)").bitcast(I32), y_codes[:].bitcast(I32))
+        for quad in range(4):
+            queue = nc.scalar if quad % 2 == 0 else nc.sync
+            queue.dma_start(
+                out_2[0, 4 * quad : 4 * quad + 4, :].bitcast(I32),
+                y_scales[32 * quad : 32 * quad + 4, :].bitcast(I32),
+            )

@@ -23,94 +23,113 @@ TEAM = Q // G
 HALVES = 2
 QH = Q // HALVES
 GH = G // HALVES
+UH = TEAM // HALVES
+VALS_BYTES = T * 4
 
 
 def tile_attend_teamshares_pl_kernel(tc, query, keys_words, keys_scales, reserve, us, vals, offs, out_0, out_1, out_2):
     nc = tc.nc
     with ExitStack() as ctx:
         sb = ctx.enter_context(tc.tile_pool(name="sb", bufs=1))
+        held = ctx.enter_context(tc.tile_pool(name="held", bufs=1))
         ps = ctx.enter_context(tc.psum_pool(name="ps", bufs=1))
         turn = ctx.enter_context(tc.psum_pool(name="turn", bufs=2))
 
         offsets = sb.tile([P, I // 16], U16, name="offsets")
         nc.sync.dma_start(offsets[:], offs)
 
-        pool_words = sb.tile([P, T], U16, name="pool_words", align_bytes=64)
-        nc.sync.dma_start(pool_words[:].bitcast(I32), keys_words[0].bitcast(I32))
+        reserve_sb = sb.tile([P, PACK], F32, name="reserve_sb")
+        nc.sync.dma_start(reserve_sb[:], reserve.rearrange("(p r) o -> p (r o)", r=PACK))
+        us_sb = sb.tile([P, PACK], F32, name="us_sb")
+        nc.sync.dma_start(us_sb[:], us.rearrange("(p r) o -> p (r o)", r=PACK))
 
         pool_scales = sb.tile([P, T], U8, name="pool_scales", align_bytes=64)
         nc.gpsimd.memset(pool_scales[:].bitcast(I32), 0)
-        identity = sb.tile([P, P], F32, name="identity")
-        make_identity(nc, identity[:])
-        warm_in = sb.tile([P, 8], F32, name="warm_in")
-        nc.vector.memset(warm_in[:], 0.0)
-
         for quad in range(4):
             nc.sync.dma_start(
                 pool_scales[32 * quad : 32 * quad + 4, :].bitcast(I32),
                 keys_scales[0, 4 * quad : 4 * quad + 4, :].bitcast(I32),
             )
-        q_raw = sb.tile([P, PACK, Q], F32, name="q_raw")
-        nc.sync.dma_start(q_raw[:], query.rearrange("(p j) q -> p j q", j=PACK))
+        pool_words = sb.tile([P, T], U16, name="pool_words", align_bytes=64)
+        nc.sync.dma_start(pool_words[:].bitcast(I32), keys_words[0].bitcast(I32))
+        q_rows = query.rearrange("(p j) q -> p j q", j=PACK)
+        q_raw = []
+        for h in range(HALVES):
+            tile = sb.tile([P, PACK, QH], F32, name="q_raw%d" % h)
+            nc.sync.dma_start(tile[:], q_rows[:, :, h * QH : (h + 1) * QH])
+            q_raw.append(tile)
         vals_rows = vals.rearrange("(p j) t -> j p t", j=PACK)
-        pool_vals = [sb.tile([P, T], F32, name="pool_vals%d" % j, align_bytes=64) for j in range(PACK)]
-        reserve_sb = sb.tile([P, PACK], F32, name="reserve_sb")
-        us_sb = sb.tile([P, PACK], F32, name="us_sb")
-        nc.sync.dma_start(pool_vals[0][:], vals_rows[0])
-        nc.sync.dma_start(reserve_sb[:], reserve.rearrange("(p r) o -> p (r o)", r=PACK))
-        nc.sync.dma_start(us_sb[:], us.rearrange("(p r) o -> p (r o)", r=PACK))
-        for j in range(1, PACK):
+        pool_vals = [held.tile([P, T], F32, name="pool_vals%d" % j, offset=j * VALS_BYTES, align_bytes=64) for j in range(PACK)]
+        for j in range(PACK):
             nc.sync.dma_start(pool_vals[j][:], vals_rows[j])
 
+        def after_gather(j, shape, dtype, name, at=0):
+            return held.tile(shape, dtype, name=name, offset=j * VALS_BYTES + at, align_bytes=64)
+
+        identity = sb.tile([P, P], F32, name="identity")
+        make_identity(nc, identity[:])
+        warm_in = sb.tile([P, 8], F32, name="warm_in")
+        nc.vector.memset(warm_in[:], 0.0)
         warm_out = sb.tile([P, 8], F32, name="warm_out")
         nc.scalar.activation(warm_out[:], warm_in[:], EXP)
 
         got_scales = sb.tile([P, I], U8, name="got_scales", align_bytes=64)
         nc.vector.tensor_copy(got_scales[:], pool_scales[:].indirect(offsets[:]))
-        got_words = sb.tile([P, I], U16, name="got_words", align_bytes=64)
-        nc.vector.tensor_copy(got_words[:], pool_words[:].indirect(offsets[:]))
         k_scales = sb.tile([P, I], U8, name="k_scales", align_bytes=64)
         nc.vector.tensor_copy(
             k_scales[:].rearrange("p (r s) -> p s r", r=PACK), got_scales[:].rearrange("p (s r) -> p s r", r=PACK)
         )
+        got_words = sb.tile([P, I], U16, name="got_words", align_bytes=64)
+        nc.vector.tensor_copy(got_words[:], pool_words[:].indirect(offsets[:]))
         k_words = sb.tile([P, I], U16, name="k_words", align_bytes=64)
         nc.vector.tensor_copy(
             k_words[:].rearrange("p (r s) -> p s r", r=PACK), got_words[:].rearrange("p (s r) -> p s r", r=PACK)
         )
 
-        q_bf = sb.tile([P, Q, PACK], BF16, name="q_bf", align_bytes=64)
-        nc.scalar.copy(q_bf[:], q_raw[:].rearrange("p j q -> p q j"))
-        q_codes = sb.tile([P, Q], U32, name="q_codes", align_bytes=64)
-        q_scales = sb.tile([P, Q], U8, name="q_scales", align_bytes=64)
-        nc.vector.quantize_mx(q_codes[:].bitcast(FP8X4), q_scales[:], q_bf[:].rearrange("p q j -> p (q j)"))
-
-        reserve_wide = sb.tile([P, G, PACK], F32, name="reserve_wide")
-        nc.scalar.copy(reserve_wide[:], reserve_sb[:].unsqueeze(1).to_broadcast([P, G, PACK]))
+        reserve_wide = sb.tile([P, G, PACK], F32, name="reserve_wide", align_bytes=64)
+        nc.gpsimd.tensor_copy(reserve_wide[:], reserve_sb[:].unsqueeze(1).to_broadcast([P, G, PACK]))
 
         p_sb = sb.tile([P, TEAM, G * PACK], F32, name="p_sb", align_bytes=64)
+        q_bf = [sb.tile([P, QH, PACK], BF16, name="q_bf%d" % h, align_bytes=64) for h in range(HALVES)]
+        for c in range(HALVES):
+            for h in range(HALVES):
+                nc.scalar.copy(
+                    q_bf[h][:].rearrange("p (u g) j -> p g u j", u=UH)[:, c * GH : (c + 1) * GH],
+                    q_raw[c][:].rearrange("p j (g u) -> p g u j", u=TEAM)[:, :, h * UH : (h + 1) * UH, :],
+                )
+        q_ops = []
+        for h in range(HALVES):
+            q_codes = sb.tile([P, QH], U32, name="q_codes%d" % h, align_bytes=64)
+            q_scales = sb.tile([P, QH], U8, name="q_scales%d" % h, align_bytes=64)
+            nc.vector.quantize_mx(q_codes[:].bitcast(FP8X4), q_scales[:], q_bf[h][:].rearrange("p q j -> p (q j)"))
+            q_ops.append((q_codes, q_scales))
         for h in range(HALVES):
             scores = ps.tile([P, PACK, QH], F32, name="scores%d" % h)
-            cols = slice(h * QH, (h + 1) * QH)
             for r in range(PACK):
                 slots = slice(r * P, (r + 1) * P)
                 nc.tensor.matmul_mx(
                     scores[:, r, :],
                     lhsT=k_words[:, slots].bitcast(FP4X4),
                     lhsT_scale=k_scales[:, slots],
-                    rhs=q_codes[:, cols].bitcast(FP8X4),
-                    rhs_scale=q_scales[:, cols],
+                    rhs=q_ops[h][0][:].bitcast(FP8X4),
+                    rhs_scale=q_ops[h][1][:],
                     start=True,
                     stop=True,
                 )
-            nc.scalar.activation(
-                p_sb[:, :, h * GH * PACK : (h + 1) * GH * PACK].rearrange("p u (g r) -> p u g r", r=PACK),
-                scores[:].rearrange("p r (g u) -> p u g r", u=TEAM),
-                EXP,
-            )
+            for pair in range(UH // 2):
+                first = h * UH + 2 * pair
+                nc.scalar.activation(
+                    p_sb[:, first : first + 2, :].rearrange("p u (g r) -> p (u g) r", r=PACK),
+                    scores[:, :, 2 * pair * G : 2 * (pair + 1) * G].rearrange("p r c -> p c r"),
+                    EXP,
+                )
 
-        def gather_and_turn(j):
+        def gather_vals(j):
             got = sb.tile([P, I], BF16, name="got_vals%d" % j, align_bytes=64)
             nc.vector.tensor_copy(got[:], pool_vals[j][:].indirect(offsets[:]))
+            return got
+
+        def turn_vals(j, got):
             pairs = got[:].bitcast(F32)
             turned = turn.tile([P, 2, P], F32, name="turned")
             for u in range(2):
@@ -123,13 +142,13 @@ def tile_attend_teamshares_pl_kernel(tc, query, keys_words, keys_scales, reserve
             return v_bf
 
         def quantize_vals(j, v_bf):
-            codes = sb.tile([P, P], U32, name="v_codes%d" % j, align_bytes=64)
+            if j < 2:
+                codes = after_gather(2, [P, P], U32, "v_codes%d" % j, at=(j + 1) * P * 4)
+            else:
+                codes = sb.tile([P, P], U32, name="v_codes%d" % j, align_bytes=64)
             scales = sb.tile([P, P], U8, name="v_scales%d" % j, align_bytes=64)
             nc.vector.quantize_mx(codes[:].bitcast(FP8X4), scales[:], v_bf[:].rearrange("p m t -> p (m t)"))
             return codes, scales
-
-        v_ops = []
-        v_bf0 = gather_and_turn(0)
 
         den_t = ps.tile([P, P], F32, name="den_t")
         nc.tensor.matmul(
@@ -137,71 +156,77 @@ def tile_attend_teamshares_pl_kernel(tc, query, keys_words, keys_scales, reserve
         )
         for u in range(TEAM):
             nc.tensor.matmul(den_t[:], p_sb[:, u, :], identity[:], start=False, stop=(u == TEAM - 1), is_transpose=True)
-        v_ops.append(quantize_vals(0, v_bf0))
-        rec_t = sb.tile([P, P], F32, name="rec_t")
+
+        v_bf0 = turn_vals(0, gather_vals(0))
+        v_bf1 = turn_vals(1, gather_vals(1))
+        rec_t = after_gather(1, [P, P], F32, "rec_t")
         nc.vector.reciprocal(rec_t[:], den_t[:])
         rec = ps.tile([P, P], F32, name="rec")
         nc.tensor.transpose(rec[:], rec_t[:], identity[:])
-        v_bf1 = gather_and_turn(1)
-        b_sb = sb.tile([P, G, PACK], F32, name="b_sb")
+        v_bf2 = turn_vals(2, gather_vals(2))
+        b_sb = after_gather(2, [P, G, PACK], F32, "b_sb")
         nc.vector.tensor_tensor(
             b_sb[:],
             rec[:].rearrange("p (g r) -> p g r", r=PACK),
             us_sb[:].unsqueeze(1).to_broadcast([P, G, PACK]),
             MULT,
         )
-        v_ops.append(quantize_vals(1, v_bf1))
+        v_ops = [quantize_vals(0, v_bf0), quantize_vals(1, v_bf1)]
 
-        w_bf, w_codes, w_scales = [], [], []
-        for h in range(HALVES):
+        def weights(h, w_bf):
             part = slice(h * GH * PACK, (h + 1) * GH * PACK)
-            w_h = sb.tile([P, TEAM, GH * PACK], BF16, name="w_bf%d" % h, align_bytes=64)
             nc.vector.tensor_tensor(
-                w_h[:],
+                w_bf[:],
                 p_sb[:, :, part],
                 b_sb[:].rearrange("p g r -> p (g r)")[:, part].unsqueeze(1).to_broadcast([P, TEAM, GH * PACK]),
                 MULT,
             )
-            w_bf.append(w_h)
-        for h in range(HALVES):
+
+        def quantize_weights(h, w_bf):
             codes = sb.tile([P, QH], U32, name="w_codes%d" % h, align_bytes=64)
             scales = sb.tile([P, QH], U8, name="w_scales%d" % h, align_bytes=64)
-            nc.vector.quantize_mx(codes[:].bitcast(FP8X4), scales[:], w_bf[h][:].rearrange("p u x -> p (u x)"))
-            w_codes.append(codes)
-            w_scales.append(scales)
-
-        v_ops.append(quantize_vals(2, gather_and_turn(2)))
+            nc.vector.quantize_mx(codes[:].bitcast(FP8X4), scales[:], w_bf[:].rearrange("p u x -> p (u x)"))
+            return codes, scales
 
         sums = [ps.tile([P, PACK, QH], F32, name="sums%d" % h) for h in range(HALVES)]
         out_rows = out_0.rearrange("(p j) q -> p j q", j=PACK)
 
-        def product(j):
-            for h in range(HALVES):
-                nc.tensor.matmul_mx(
-                    sums[h][:, j, :],
-                    lhsT=v_ops[j][0][:].bitcast(FP8X4),
-                    lhsT_scale=v_ops[j][1][:],
-                    rhs=w_codes[h][:].bitcast(FP8X4),
-                    rhs_scale=w_scales[h][:],
-                    start=True,
-                    stop=True,
-                )
+        def product(j, h):
+            nc.tensor.matmul_mx(
+                sums[h][:, j, :],
+                lhsT=v_ops[j][0][:].bitcast(FP8X4),
+                lhsT_scale=v_ops[j][1][:],
+                rhs=w_ops[h][0][:].bitcast(FP8X4),
+                rhs_scale=w_ops[h][1][:],
+                start=True,
+                stop=True,
+            )
 
-        def store_rows(first, count):
-            o_sb = sb.tile([P, count, Q], F32, name="o_sb%d" % first)
-            for h in range(HALVES):
-                nc.scalar.copy(
-                    o_sb[:, :, h * QH : (h + 1) * QH].rearrange("p j (g u) -> p j g u", u=TEAM),
-                    sums[h][:, first : first + count, :].rearrange("p j (u g) -> p j g u", u=TEAM),
-                )
-            nc.sync.dma_start(out_rows[:, first : first + count, :], o_sb[:])
+        def store_rows(h, first, count, copy, queue):
+            o_sb = sb.tile([P, count, QH], F32, name="o_sb%d_%d" % (h, first))
+            copy(
+                o_sb[:].rearrange("p j (g u) -> p j g u", u=TEAM),
+                sums[h][:, first : first + count, :].rearrange("p j (u g) -> p j g u", u=TEAM),
+            )
+            queue.dma_start(out_rows[:, first : first + count, h * QH : (h + 1) * QH], o_sb[:])
 
+        w_bf0 = sb.tile([P, TEAM, GH * PACK], BF16, name="w_bf0", align_bytes=64)
+        weights(0, w_bf0)
+        v_ops.append(quantize_vals(2, v_bf2))
+        w_ops = [quantize_weights(0, w_bf0)]
         for j in range(PACK - 1):
-            product(j)
-        store_rows(0, PACK - 1)
+            product(j, 0)
+        store_rows(0, 0, PACK - 1, nc.scalar.copy, nc.sync)
 
-        v_ops.append(quantize_vals(3, gather_and_turn(3)))
-        product(PACK - 1)
+        v_bf3 = turn_vals(3, gather_vals(3))
+        w_bf1 = after_gather(3, [P, TEAM, GH * PACK], BF16, "w_bf1")
+        weights(1, w_bf1)
+        w_ops.append(quantize_weights(1, w_bf1))
+        v_ops.append(quantize_vals(3, v_bf3))
+        for j in range(PACK - 1):
+            product(j, 1)
+        for h in range(HALVES):
+            product(PACK - 1, h)
 
         y_bf = sb.tile([P, Q, PACK], BF16, name="y_bf", align_bytes=64)
         for h, copy in enumerate((nc.vector.tensor_copy, nc.scalar.copy)):
@@ -209,13 +234,14 @@ def tile_attend_teamshares_pl_kernel(tc, query, keys_words, keys_scales, reserve
                 y_bf[:, h * QH : (h + 1) * QH, :].rearrange("p (g u) j -> p g u j", u=TEAM),
                 sums[h][:].rearrange("p j (u g) -> p g u j", u=TEAM),
             )
-        store_rows(PACK - 1, 1)
+        store_rows(0, PACK - 1, 1, nc.vector.tensor_copy, nc.sync)
+        store_rows(1, 0, PACK, nc.scalar.copy, nc.scalar)
         y_codes = sb.tile([P, Q], U32, name="y_codes", align_bytes=64)
         y_scales = sb.tile([P, Q], U8, name="y_scales", align_bytes=64)
         nc.vector.quantize_mx(y_codes[:].bitcast(FP8X4), y_scales[:], y_bf[:].rearrange("p q j -> p (q j)"))
         nc.sync.dma_start(out_1[0].rearrange("p q j -> p (q j)").bitcast(I32), y_codes[:].bitcast(I32))
         for quad in range(4):
-            queue = nc.scalar if quad % 2 == 0 else nc.sync
+            queue = nc.scalar if quad % 2 == 1 else nc.sync
             queue.dma_start(
                 out_2[0, 4 * quad : 4 * quad + 4, :].bitcast(I32),
                 y_scales[32 * quad : 32 * quad + 4, :].bitcast(I32),

@@ -35,32 +35,27 @@ def tile_attend_teamshares_pl_kernel(tc, query, keys_words, keys_scales, reserve
         ps = ctx.enter_context(tc.psum_pool(name="ps", bufs=1))
         turn = ctx.enter_context(tc.psum_pool(name="turn", bufs=2))
 
+        pool_words = sb.tile([P, T], U16, name="pool_words", align_bytes=64)
+        nc.sync.dma_start(pool_words[:].bitcast(I32), keys_words[0].bitcast(I32))
         offsets = sb.tile([P, I // 16], U16, name="offsets")
         nc.sync.dma_start(offsets[:], offs)
-
-        reserve_sb = sb.tile([P, PACK], F32, name="reserve_sb")
-        nc.sync.dma_start(reserve_sb[:], reserve.rearrange("(p r) o -> p (r o)", r=PACK))
-        us_sb = sb.tile([P, PACK], F32, name="us_sb")
-        nc.sync.dma_start(us_sb[:], us.rearrange("(p r) o -> p (r o)", r=PACK))
-
-        pool_scales = sb.tile([P, T], U8, name="pool_scales", align_bytes=64)
+        pool_scales = sb.tile([P, T], U8, name="pool_scales", tag="pool_scales", align_bytes=64)
         nc.gpsimd.memset(pool_scales[:].bitcast(I32), 0)
         for quad in range(4):
             nc.sync.dma_start(
                 pool_scales[32 * quad : 32 * quad + 4, :].bitcast(I32),
                 keys_scales[0, 4 * quad : 4 * quad + 4, :].bitcast(I32),
             )
-        pool_words = sb.tile([P, T], U16, name="pool_words", align_bytes=64)
-        nc.sync.dma_start(pool_words[:].bitcast(I32), keys_words[0].bitcast(I32))
-        q_rows = query.rearrange("(p j) q -> p j q", j=PACK)
-        q_raw = []
-        for h in range(HALVES):
-            tile = sb.tile([P, PACK, QH], F32, name="q_raw%d" % h)
-            nc.sync.dma_start(tile[:], q_rows[:, :, h * QH : (h + 1) * QH])
-            q_raw.append(tile)
+        q_raw = sb.tile([P, PACK, Q], F32, name="q_raw")
+        nc.sync.dma_start(q_raw[:], query.rearrange("(p j) q -> p j q", j=PACK))
         vals_rows = vals.rearrange("(p j) t -> j p t", j=PACK)
         pool_vals = [held.tile([P, T], F32, name="pool_vals%d" % j, offset=j * VALS_BYTES, align_bytes=64) for j in range(PACK)]
-        for j in range(PACK):
+        nc.sync.dma_start(pool_vals[0][:], vals_rows[0])
+        reserve_sb = sb.tile([P, PACK], F32, name="reserve_sb")
+        nc.sync.dma_start(reserve_sb[:], reserve.rearrange("(p r) o -> p (r o)", r=PACK))
+        us_sb = sb.tile([P, PACK], F32, name="us_sb")
+        nc.sync.dma_start(us_sb[:], us.rearrange("(p r) o -> p (r o)", r=PACK))
+        for j in range(1, PACK):
             nc.sync.dma_start(pool_vals[j][:], vals_rows[j])
 
         def after_gather(j, shape, dtype, name, at=0):
@@ -73,17 +68,19 @@ def tile_attend_teamshares_pl_kernel(tc, query, keys_words, keys_scales, reserve
         warm_out = sb.tile([P, 8], F32, name="warm_out")
         nc.scalar.activation(warm_out[:], warm_in[:], EXP)
 
-        got_scales = sb.tile([P, I], U8, name="got_scales", align_bytes=64)
-        nc.vector.tensor_copy(got_scales[:], pool_scales[:].indirect(offsets[:]))
-        k_scales = sb.tile([P, I], U8, name="k_scales", align_bytes=64)
-        nc.vector.tensor_copy(
-            k_scales[:].rearrange("p (r s) -> p s r", r=PACK), got_scales[:].rearrange("p (s r) -> p s r", r=PACK)
-        )
         got_words = sb.tile([P, I], U16, name="got_words", align_bytes=64)
         nc.vector.tensor_copy(got_words[:], pool_words[:].indirect(offsets[:]))
-        k_words = sb.tile([P, I], U16, name="k_words", align_bytes=64)
+        got_scales = sb.tile([P, I], U8, name="got_scales", align_bytes=64)
+        nc.vector.tensor_copy(got_scales[:], pool_scales[:].indirect(offsets[:]))
+        k_words = sb.tile([P, I], U16, name="k_words", tag="pool_scales", align_bytes=64)
         nc.vector.tensor_copy(
-            k_words[:].rearrange("p (r s) -> p s r", r=PACK), got_words[:].rearrange("p (s r) -> p s r", r=PACK)
+            k_words[:].rearrange("p (r a s) -> p a r s", r=PACK, s=8),
+            got_words[:].rearrange("p (a s r) -> p a r s", r=PACK, s=8),
+        )
+        k_scales = sb.tile([P, I], U8, name="k_scales", align_bytes=64)
+        nc.vector.tensor_copy(
+            k_scales[:].rearrange("p (r a s) -> p a r s", r=PACK, s=16),
+            got_scales[:].rearrange("p (a s r) -> p a r s", r=PACK, s=16),
         )
 
         reserve_wide = sb.tile([P, G, PACK], F32, name="reserve_wide", align_bytes=64)
@@ -91,12 +88,11 @@ def tile_attend_teamshares_pl_kernel(tc, query, keys_words, keys_scales, reserve
 
         p_sb = sb.tile([P, TEAM, G * PACK], F32, name="p_sb", align_bytes=64)
         q_bf = [sb.tile([P, QH, PACK], BF16, name="q_bf%d" % h, align_bytes=64) for h in range(HALVES)]
-        for c in range(HALVES):
-            for h in range(HALVES):
-                nc.scalar.copy(
-                    q_bf[h][:].rearrange("p (u g) j -> p g u j", u=UH)[:, c * GH : (c + 1) * GH],
-                    q_raw[c][:].rearrange("p j (g u) -> p g u j", u=TEAM)[:, :, h * UH : (h + 1) * UH, :],
-                )
+        for h in range(HALVES):
+            nc.scalar.copy(
+                q_bf[h][:].rearrange("p (u g) j -> p g u j", u=UH),
+                q_raw[:].rearrange("p j (g u) -> p g u j", u=TEAM)[:, :, h * UH : (h + 1) * UH, :],
+            )
         q_ops = []
         for h in range(HALVES):
             q_codes = sb.tile([P, QH], U32, name="q_codes%d" % h, align_bytes=64)
@@ -129,25 +125,19 @@ def tile_attend_teamshares_pl_kernel(tc, query, keys_words, keys_scales, reserve
             nc.vector.tensor_copy(got[:], pool_vals[j][:].indirect(offsets[:]))
             return got
 
-        def turn_vals(j, got):
+        def turn_vals(got, v_bf):
             pairs = got[:].bitcast(F32)
             turned = turn.tile([P, 2, P], F32, name="turned")
             for u in range(2):
                 nc.tensor.transpose(turned[:, u, :], pairs[:, u : I // 2 : 2], identity[:])
-            v_bf = sb.tile([P, P, PACK], BF16, name="v_bf%d" % j, align_bytes=64)
             nc.scalar.copy(
-                v_bf[:].rearrange("p m t -> p (m t)").bitcast(F32).rearrange("p (m u) -> p m u", u=2),
+                v_bf.bitcast(F32).rearrange("p (m u) -> p m u", u=2),
                 turned[:].rearrange("p u m -> p m u"),
             )
-            return v_bf
 
-        def quantize_vals(j, v_bf):
-            if j < 2:
-                codes = after_gather(2, [P, P], U32, "v_codes%d" % j, at=(j + 1) * P * 4)
-            else:
-                codes = sb.tile([P, P], U32, name="v_codes%d" % j, align_bytes=64)
-            scales = sb.tile([P, P], U8, name="v_scales%d" % j, align_bytes=64)
-            nc.vector.quantize_mx(codes[:].bitcast(FP8X4), scales[:], v_bf[:].rearrange("p m t -> p (m t)"))
+        def quantize(name, values, codes):
+            scales = sb.tile([P, values.shape[1] // PACK], U8, name=name, align_bytes=64)
+            nc.vector.quantize_mx(codes[:].bitcast(FP8X4), scales[:], values)
             return codes, scales
 
         den_t = ps.tile([P, P], F32, name="den_t")
@@ -157,13 +147,15 @@ def tile_attend_teamshares_pl_kernel(tc, query, keys_words, keys_scales, reserve
         for u in range(TEAM):
             nc.tensor.matmul(den_t[:], p_sb[:, u, :], identity[:], start=False, stop=(u == TEAM - 1), is_transpose=True)
 
-        v_bf0 = turn_vals(0, gather_vals(0))
-        v_bf1 = turn_vals(1, gather_vals(1))
+        v_bf01 = sb.tile([P, 2, I], BF16, name="v_bf01", align_bytes=64)
+        for j in range(2):
+            turn_vals(gather_vals(j), v_bf01[:, j, :])
         rec_t = after_gather(1, [P, P], F32, "rec_t")
         nc.vector.reciprocal(rec_t[:], den_t[:])
         rec = ps.tile([P, P], F32, name="rec")
         nc.tensor.transpose(rec[:], rec_t[:], identity[:])
-        v_bf2 = turn_vals(2, gather_vals(2))
+        v_bf2 = sb.tile([P, I], BF16, name="v_bf2", align_bytes=64)
+        turn_vals(gather_vals(2), v_bf2[:])
         b_sb = after_gather(2, [P, G, PACK], F32, "b_sb")
         nc.vector.tensor_tensor(
             b_sb[:],
@@ -171,22 +163,25 @@ def tile_attend_teamshares_pl_kernel(tc, query, keys_words, keys_scales, reserve
             us_sb[:].unsqueeze(1).to_broadcast([P, G, PACK]),
             MULT,
         )
-        v_ops = [quantize_vals(0, v_bf0), quantize_vals(1, v_bf1)]
+        v01 = quantize(
+            "v_scales01", v_bf01[:].rearrange("p j x -> p (j x)"), after_gather(2, [P, 2 * P], U32, "v_codes01", at=P * 4)
+        )
+        v_ops = [(v01[0][:, j * P : (j + 1) * P], v01[1][:, j * P : (j + 1) * P]) for j in range(2)]
 
-        def weights(h, w_bf):
+        w_bf = sb.tile([P, HALVES, TEAM, GH * PACK], BF16, name="w_bf", align_bytes=64)
+        for h in range(HALVES):
             part = slice(h * GH * PACK, (h + 1) * GH * PACK)
             nc.vector.tensor_tensor(
-                w_bf[:],
+                w_bf[:, h],
                 p_sb[:, :, part],
                 b_sb[:].rearrange("p g r -> p (g r)")[:, part].unsqueeze(1).to_broadcast([P, TEAM, GH * PACK]),
                 MULT,
             )
-
-        def quantize_weights(h, w_bf):
-            codes = sb.tile([P, QH], U32, name="w_codes%d" % h, align_bytes=64)
-            scales = sb.tile([P, QH], U8, name="w_scales%d" % h, align_bytes=64)
-            nc.vector.quantize_mx(codes[:].bitcast(FP8X4), scales[:], w_bf[:].rearrange("p u x -> p (u x)"))
-            return codes, scales
+        v2 = quantize("v_scales2", v_bf2[:], sb.tile([P, P], U32, name="v_codes2", align_bytes=64))
+        v_ops.append((v2[0][:], v2[1][:]))
+        w_codes, w_scales = quantize(
+            "w_scales", w_bf[:].rearrange("p h u x -> p (h u x)"), sb.tile([P, Q], U32, name="w_codes", align_bytes=64)
+        )
 
         sums = [ps.tile([P, PACK, QH], F32, name="sums%d" % h) for h in range(HALVES)]
         out_rows = out_0.rearrange("(p j) q -> p j q", j=PACK)
@@ -194,39 +189,34 @@ def tile_attend_teamshares_pl_kernel(tc, query, keys_words, keys_scales, reserve
         def product(j, h):
             nc.tensor.matmul_mx(
                 sums[h][:, j, :],
-                lhsT=v_ops[j][0][:].bitcast(FP8X4),
-                lhsT_scale=v_ops[j][1][:],
-                rhs=w_ops[h][0][:].bitcast(FP8X4),
-                rhs_scale=w_ops[h][1][:],
+                lhsT=v_ops[j][0].bitcast(FP8X4),
+                lhsT_scale=v_ops[j][1],
+                rhs=w_codes[:, h * QH : (h + 1) * QH].bitcast(FP8X4),
+                rhs_scale=w_scales[:, h * QH : (h + 1) * QH],
                 start=True,
                 stop=True,
             )
 
-        def store_rows(h, first, count, copy, queue):
-            o_sb = sb.tile([P, count, QH], F32, name="o_sb%d_%d" % (h, first))
-            copy(
-                o_sb[:].rearrange("p j (g u) -> p j g u", u=TEAM),
-                sums[h][:, first : first + count, :].rearrange("p j (u g) -> p j g u", u=TEAM),
-            )
-            queue.dma_start(out_rows[:, first : first + count, h * QH : (h + 1) * QH], o_sb[:])
+        def store_rows(first, o_sb, copies):
+            count = o_sb.shape[1]
+            for h in range(HALVES):
+                copies[h](
+                    o_sb[:, :, h * QH : (h + 1) * QH].rearrange("p j (g u) -> p j g u", u=TEAM),
+                    sums[h][:, first : first + count, :].rearrange("p j (u g) -> p j g u", u=TEAM),
+                )
+            nc.sync.dma_start(out_rows[:, first : first + count, :], o_sb[:])
 
-        w_bf0 = sb.tile([P, TEAM, GH * PACK], BF16, name="w_bf0", align_bytes=64)
-        weights(0, w_bf0)
-        v_ops.append(quantize_vals(2, v_bf2))
-        w_ops = [quantize_weights(0, w_bf0)]
-        for j in range(PACK - 1):
-            product(j, 0)
-        store_rows(0, 0, PACK - 1, nc.scalar.copy, nc.sync)
-
-        v_bf3 = turn_vals(3, gather_vals(3))
-        w_bf1 = after_gather(3, [P, TEAM, GH * PACK], BF16, "w_bf1")
-        weights(1, w_bf1)
-        w_ops.append(quantize_weights(1, w_bf1))
-        v_ops.append(quantize_vals(3, v_bf3))
-        for j in range(PACK - 1):
-            product(j, 1)
         for h in range(HALVES):
-            product(PACK - 1, h)
+            for j in range(PACK - 1):
+                product(j, h)
+        v_bf3 = sb.tile([P, I], BF16, name="v_bf3", align_bytes=64)
+        turn_vals(gather_vals(3), v_bf3[:])
+        o_first = after_gather(3, [P, PACK - 1, Q], F32, "o_first")
+        store_rows(0, o_first, (nc.vector.tensor_copy, nc.vector.tensor_copy))
+        v3 = quantize("v_scales3", v_bf3[:], sb.tile([P, P], U32, name="v_codes3", align_bytes=64))
+        v_ops.append((v3[0][:], v3[1][:]))
+        for h in range(HALVES):
+            product(3, h)
 
         y_bf = sb.tile([P, Q, PACK], BF16, name="y_bf", align_bytes=64)
         for h, copy in enumerate((nc.vector.tensor_copy, nc.scalar.copy)):
@@ -234,8 +224,8 @@ def tile_attend_teamshares_pl_kernel(tc, query, keys_words, keys_scales, reserve
                 y_bf[:, h * QH : (h + 1) * QH, :].rearrange("p (g u) j -> p g u j", u=TEAM),
                 sums[h][:].rearrange("p j (u g) -> p g u j", u=TEAM),
             )
-        store_rows(0, PACK - 1, 1, nc.vector.tensor_copy, nc.sync)
-        store_rows(1, 0, PACK, nc.scalar.copy, nc.scalar)
+        o_last = sb.tile([P, 1, Q], F32, name="o_last")
+        store_rows(3, o_last, (nc.vector.tensor_copy, nc.scalar.copy))
         y_codes = sb.tile([P, Q], U32, name="y_codes", align_bytes=64)
         y_scales = sb.tile([P, Q], U8, name="y_scales", align_bytes=64)
         nc.vector.quantize_mx(y_codes[:].bitcast(FP8X4), y_scales[:], y_bf[:].rearrange("p q j -> p (q j)"))

from contextlib import ExitStack

import concourse.mybir as mybir
from concourse.masks import make_identity

D, T, I, Q, G, E = 512, 2048, 512, 256, 32, 512
FLOPS = 2 * D * I * Q + 2 * I * E * Q

F32 = mybir.dt.float32
BF16 = mybir.dt.bfloat16
I32 = mybir.dt.int32
U32 = mybir.dt.uint32
U16 = mybir.dt.uint16
U8 = mybir.dt.uint8
FP8X4 = mybir.dt.float8_e4m3fn_x4
FP4X4 = mybir.dt.float4_e2m1fn_x4
EXP = mybir.ActivationFunctionType.Exp
MULT = mybir.AluOpType.mult

P = 128
PACK = 4
TEAM = Q // G
HALVES = 2
QH = Q // HALVES
GH = G // HALVES
UH = TEAM // HALVES
VALS_BYTES = T * 4


def tile_attend_teamshares_pl_kernel(tc, query, keys_words, keys_scales, reserve, us, vals, offs, out_0, out_1, out_2):
    nc = tc.nc
    with ExitStack() as ctx:
        sb = ctx.enter_context(tc.tile_pool(name="sb", bufs=1))
        held = ctx.enter_context(tc.tile_pool(name="held", bufs=1))
        ps = ctx.enter_context(tc.psum_pool(name="ps", bufs=1))
        turn = ctx.enter_context(tc.psum_pool(name="turn", bufs=2))

        pool_words = sb.tile([P, T], U16, name="pool_words", align_bytes=64)
        nc.sync.dma_start(pool_words[:].bitcast(I32), keys_words[0].bitcast(I32))
        offsets = sb.tile([P, I // 16], U16, name="offsets")
        nc.sync.dma_start(offsets[:], offs)
        pool_scales = sb.tile([P, T], U8, name="pool_scales", tag="pool_scales", align_bytes=64)
        nc.gpsimd.memset(pool_scales[:].bitcast(I32), 0)
        for quad in range(4):
            nc.sync.dma_start(
                pool_scales[32 * quad : 32 * quad + 4, :].bitcast(I32),
                keys_scales[0, 4 * quad : 4 * quad + 4, :].bitcast(I32),
            )
        q_raw = sb.tile([P, PACK, Q], F32, name="q_raw")
        nc.sync.dma_start(q_raw[:], query.rearrange("(p j) q -> p j q", j=PACK))
        vals_rows = vals.rearrange("(p j) t -> j p t", j=PACK)
        pool_vals = [held.tile([P, T], F32, name="pool_vals%d" % j, offset=j * VALS_BYTES, align_bytes=64) for j in range(PACK)]
        nc.sync.dma_start(pool_vals[0][:], vals_rows[0])
        reserve_sb = sb.tile([P, PACK], F32, name="reserve_sb")
        nc.sync.dma_start(reserve_sb[:], reserve.rearrange("(p r) o -> p (r o)", r=PACK))
        us_sb = sb.tile([P, PACK], F32, name="us_sb")
        nc.sync.dma_start(us_sb[:], us.rearrange("(p r) o -> p (r o)", r=PACK))
        for j in range(1, PACK):
            nc.sync.dma_start(pool_vals[j][:], vals_rows[j])

        def after_gather(j, shape, dtype, name, at=0):
            return held.tile(shape, dtype, name=name, offset=j * VALS_BYTES + at, align_bytes=64)

        identity = sb.tile([P, P], F32, name="identity")
        make_identity(nc, identity[:])
        warm_in = sb.tile([P, 8], F32, name="warm_in")
        nc.vector.memset(warm_in[:], 0.0)
        warm_out = sb.tile([P, 8], F32, name="warm_out")
        nc.scalar.activation(warm_out[:], warm_in[:], EXP)

        got_words = sb.tile([P, I], U16, name="got_words", align_bytes=64)
        nc.vector.tensor_copy(got_words[:], pool_words[:].indirect(offsets[:]))
        got_scales = sb.tile([P, I], U8, name="got_scales", align_bytes=64)
        nc.vector.tensor_copy(got_scales[:], pool_scales[:].indirect(offsets[:]))
        k_words = sb.tile([P, I], U16, name="k_words", tag="pool_scales", align_bytes=64)
        nc.vector.tensor_copy(
            k_words[:].rearrange("p (r a s) -> p a r s", r=PACK, s=8),
            got_words[:].rearrange("p (a s r) -> p a r s", r=PACK, s=8),
        )
        k_scales = sb.tile([P, I], U8, name="k_scales", align_bytes=64)
        nc.vector.tensor_copy(
            k_scales[:].rearrange("p (r a s) -> p a r s", r=PACK, s=16),
            got_scales[:].rearrange("p (a s r) -> p a r s", r=PACK, s=16),
        )

        reserve_wide = sb.tile([P, G, PACK], F32, name="reserve_wide", align_bytes=64)
        nc.gpsimd.tensor_copy(reserve_wide[:], reserve_sb[:].unsqueeze(1).to_broadcast([P, G, PACK]))

        p_sb = sb.tile([P, TEAM, G * PACK], F32, name="p_sb", align_bytes=64)
        q_bf = [sb.tile([P, QH, PACK], BF16, name="q_bf%d" % h, align_bytes=64) for h in range(HALVES)]
        for h in range(HALVES):
            nc.scalar.copy(
                q_bf[h][:].rearrange("p (u g) j -> p g u j", u=UH),
                q_raw[:].rearrange("p j (g u) -> p g u j", u=TEAM)[:, :, h * UH : (h + 1) * UH, :],
            )
        q_ops = []
        for h in range(HALVES):
            q_codes = sb.tile([P, QH], U32, name="q_codes%d" % h, align_bytes=64)
            q_scales = sb.tile([P, QH], U8, name="q_scales%d" % h, align_bytes=64)
            nc.vector.quantize_mx(q_codes[:].bitcast(FP8X4), q_scales[:], q_bf[h][:].rearrange("p q j -> p (q j)"))
            q_ops.append((q_codes, q_scales))
        for h in range(HALVES):
            scores = ps.tile([P, PACK, QH], F32, name="scores%d" % h)
            for r in range(PACK):
                slots = slice(r * P, (r + 1) * P)
                nc.tensor.matmul_mx(
                    scores[:, r, :],
                    lhsT=k_words[:, slots].bitcast(FP4X4),
                    lhsT_scale=k_scales[:, slots],
                    rhs=q_ops[h][0][:].bitcast(FP8X4),
                    rhs_scale=q_ops[h][1][:],
                    start=True,
                    stop=True,
                )
            for pair in range(UH // 2):
                first = h * UH + 2 * pair
                nc.scalar.activation(
                    p_sb[:, first : first + 2, :].rearrange("p u (g r) -> p (u g) r", r=PACK),
                    scores[:, :, 2 * pair * G : 2 * (pair + 1) * G].rearrange("p r c -> p c r"),
                    EXP,
                )

        def gather_vals(j):
            got = sb.tile([P, I], BF16, name="got_vals%d" % j, align_bytes=64)
            nc.vector.tensor_copy(got[:], pool_vals[j][:].indirect(offsets[:]))
            return got

        def turn_vals(got, v_bf):
            pairs = got[:].bitcast(F32)
            turned = turn.tile([P, 2, P], F32, name="turned")
            for u in range(2):
                nc.tensor.transpose(turned[:, u, :], pairs[:, u : I // 2 : 2], identity[:])
            nc.scalar.copy(
                v_bf.bitcast(F32).rearrange("p (m u) -> p m u", u=2),
                turned[:].rearrange("p u m -> p m u"),
            )

        def quantize(name, values, codes):
            scales = sb.tile([P, values.shape[1] // PACK], U8, name=name, align_bytes=64)
            nc.vector.quantize_mx(codes[:].bitcast(FP8X4), scales[:], values)
            return codes, scales

        den_t = ps.tile([P, P], F32, name="den_t")
        nc.tensor.matmul(
            den_t[:], reserve_wide[:].rearrange("p g r -> p (g r)"), identity[:], start=True, stop=False, is_transpose=True
        )
        for u in range(TEAM):
            nc.tensor.matmul(den_t[:], p_sb[:, u, :], identity[:], start=False, stop=(u == TEAM - 1), is_transpose=True)

        v_bf01 = sb.tile([P, 2, I], BF16, name="v_bf01", align_bytes=64)
        for j in range(2):
            turn_vals(gather_vals(j), v_bf01[:, j, :])
        rec_t = after_gather(1, [P, P], F32, "rec_t")
        nc.vector.reciprocal(rec_t[:], den_t[:])
        rec = ps.tile([P, P], F32, name="rec")
        nc.tensor.transpose(rec[:], rec_t[:], identity[:])
        v_bf2 = sb.tile([P, I], BF16, name="v_bf2", align_bytes=64)
        turn_vals(gather_vals(2), v_bf2[:])
        b_sb = after_gather(2, [P, G, PACK], F32, "b_sb")
        nc.vector.tensor_tensor(
            b_sb[:],
            rec[:].rearrange("p (g r) -> p g r", r=PACK),
            us_sb[:].unsqueeze(1).to_broadcast([P, G, PACK]),
            MULT,
        )
        v01 = quantize(
            "v_scales01", v_bf01[:].rearrange("p j x -> p (j x)"), after_gather(2, [P, 2 * P], U32, "v_codes01", at=P * 4)
        )
        v_ops = [(v01[0][:, j * P : (j + 1) * P], v01[1][:, j * P : (j + 1) * P]) for j in range(2)]

        w_bf = sb.tile([P, HALVES, TEAM, GH * PACK], BF16, name="w_bf", align_bytes=64)
        for h in range(HALVES):
            part = slice(h * GH * PACK, (h + 1) * GH * PACK)
            nc.vector.tensor_tensor(
                w_bf[:, h],
                p_sb[:, :, part],
                b_sb[:].rearrange("p g r -> p (g r)")[:, part].unsqueeze(1).to_broadcast([P, TEAM, GH * PACK]),
                MULT,
            )
        v2 = quantize("v_scales2", v_bf2[:], sb.tile([P, P], U32, name="v_codes2", align_bytes=64))
        v_ops.append((v2[0][:], v2[1][:]))
        w_codes, w_scales = quantize(
            "w_scales", w_bf[:].rearrange("p h u x -> p (h u x)"), sb.tile([P, Q], U32, name="w_codes", align_bytes=64)
        )

        sums = [ps.tile([P, PACK, QH], F32, name="sums%d" % h) for h in range(HALVES)]
        out_rows = out_0.rearrange("(p j) q -> p j q", j=PACK)

        def product(j, h):
            nc.tensor.matmul_mx(
                sums[h][:, j, :],
                lhsT=v_ops[j][0].bitcast(FP8X4),
                lhsT_scale=v_ops[j][1],
                rhs=w_codes[:, h * QH : (h + 1) * QH].bitcast(FP8X4),
                rhs_scale=w_scales[:, h * QH : (h + 1) * QH],
                start=True,
                stop=True,
            )

        def store_rows(first, o_sb, copies):
            count = o_sb.shape[1]
            for h in range(HALVES):
                copies[h](
                    o_sb[:, :, h * QH : (h + 1) * QH].rearrange("p j (g u) -> p j g u", u=TEAM),
                    sums[h][:, first : first + count, :].rearrange("p j (u g) -> p j g u", u=TEAM),
                )
            nc.sync.dma_start(out_rows[:, first : first + count, :], o_sb[:])

        for h in range(HALVES):
            for j in range(PACK - 1):
                product(j, h)
        v_bf3 = sb.tile([P, I], BF16, name="v_bf3", align_bytes=64)
        turn_vals(gather_vals(3), v_bf3[:])
        o_first = after_gather(3, [P, PACK - 1, Q], F32, "o_first")
        store_rows(0, o_first, (nc.vector.tensor_copy, nc.vector.tensor_copy))
        v3 = quantize("v_scales3", v_bf3[:], sb.tile([P, P], U32, name="v_codes3", align_bytes=64))
        v_ops.append((v3[0][:], v3[1][:]))
        for h in range(HALVES):
            product(3, h)

        y_bf = sb.tile([P, Q, PACK], BF16, name="y_bf", align_bytes=64)
        for h, copy in enumerate((nc.vector.tensor_copy, nc.scalar.copy)):
            copy(
                y_bf[:, h * QH : (h + 1) * QH, :].rearrange("p (g u) j -> p g u j", u=TEAM),
                sums[h][:].rearrange("p j (u g) -> p g u j", u=TEAM),
            )
        o_last = sb.tile([P, 1, Q], F32, name="o_last")
        store_rows(3, o_last, (nc.vector.tensor_copy, nc.scalar.copy))
        y_codes = sb.tile([P, Q], U32, name="y_codes", align_bytes=64)
        y_scales = sb.tile([P, Q], U8, name="y_scales", align_bytes=64)
        nc.vector.quantize_mx(y_codes[:].bitcast(FP8X4), y_scales[:], y_bf[:].rearrange("p q j -> p (q j)"))
        nc.sync.dma_start(out_1[0].rearrange("p q j -> p (q j)").bitcast(I32), y_codes[:].bitcast(I32))
        for quad in range(4):
            queue = nc.scalar if quad % 2 == 1 else nc.sync
            queue.dma_start(
                out_2[0, 4 * quad : 4 * quad + 4, :].bitcast(I32),
                y_scales[32 * quad : 32 * quad + 4, :].bitcast(I32),
            )
